import numpy as np
import ml_dtypes


def mxq(x, axis, fmt="e4m3"):
    dtype, down = {"e4m3": (ml_dtypes.float8_e4m3fn, 7), "e5m2": (ml_dtypes.float8_e5m2, 14)}[fmt]
    v = np.moveaxis(np.asarray(x, np.float32).astype(ml_dtypes.bfloat16).astype(np.float64), axis, -1)
    blocks = v.reshape(v.shape[:-1] + (-1, 32))
    amax = np.abs(blocks).max(-1, keepdims=True)
    byte = np.maximum(np.where(amax > 0, np.frexp(amax)[1] - 1 + 127, 0) - down, 1)
    scale = np.exp2(byte - 127.0)
    codes = (blocks / scale).astype(np.float32).astype(dtype).astype(np.float64)
    return np.moveaxis((codes * scale).reshape(v.shape), -1, axis)


WIDE = False


def mx_kscale(k):
    if not WIDE:
        return np.ones(k)
    levels = np.array([10, -10, 5, -5, 0])
    if k % 512:
        return np.exp2(np.random.permutation(np.resize(levels, k // 32))).repeat(32)
    a = np.empty((k // 512, 16))
    for p in range(k // 512):
        a[p, :8] = np.random.permutation(np.resize(levels, 8))
        for g in range(8):
            far = levels[np.abs(levels - a[p, g]) >= 10]
            a[p, g + 8] = far[np.random.randint(len(far))]
    return np.exp2(a.ravel()).repeat(32)


def f64(x):
    return np.asarray(x).astype(np.float64)


def striped(idx):
    return np.tile(np.asarray(idx).reshape(-1, 16).T, (8, 1)).astype(np.uint16)


def unstriped(offs):
    return offs[:16].T.reshape(-1).astype(np.int64)


def striped8(idx):
    return np.asarray(idx).reshape(8, -1, 16).transpose(0, 2, 1).reshape(128, -1).astype(np.uint16)


def unstriped8(offs):
    return offs.reshape(8, 16, -1).transpose(0, 2, 1).reshape(8, -1).astype(np.int64)


def pick8(x, idx, run):
    r = np.arange(len(x))
    return x[r[:, None], idx[r % (8 * run) // run]]


E2M1 = np.array([0.0, 0.5, 1.0, 1.5, 2.0, 3.0, 4.0, 6.0, -0.0, -0.5, -1.0, -1.5, -2.0, -3.0, -4.0, -6.0])


def pack_weight(w, fmt):
    k, n = w.shape
    w = f64(np.asarray(w, np.float32).astype(ml_dtypes.bfloat16)).reshape(k // 32, 32, n)
    amax = np.abs(w).max(1)
    if fmt == "e4m3":
        byte = np.frexp(amax)[1] - 1 + 127 - 7
    else:
        mant, ex = np.frexp(amax / 6.0)
        byte = np.where(mant > 0.5, ex, ex - 1) + 127
    byte = np.clip(np.where(amax > 0, byte, 1), 1, 254)
    scaled = (w * np.exp2(127.0 - byte)[:, None, :]).reshape(k, n).astype(np.float32)
    by_word = np.ascontiguousarray(scaled.reshape(k // 512, 128, 4, n).transpose(0, 1, 3, 2))
    if fmt == "e4m3":
        words = by_word.astype(ml_dtypes.float8_e4m3fn).view(np.uint8)
    else:
        c = by_word.astype(ml_dtypes.float4_e2m1fn).view(np.uint8) & 0xF
        words = (c[..., 0::2] | (c[..., 1::2] << 4)).reshape(k // 512, 128, 2 * n)
    return np.ascontiguousarray(words), np.ascontiguousarray(byte.astype(np.uint8).reshape(k // 512, 16, n))


def unpack_weight(words, scales, fmt):
    g, _, n = scales.shape
    words = np.ascontiguousarray(words).reshape(g, 128, n, -1)
    if fmt == "e4m3":
        vals = words.view(ml_dtypes.float8_e4m3fn).astype(np.float64)
    else:
        nib = np.empty((g, 128, n, 4), np.uint8)
        nib[..., 0::2] = words & 0xF
        nib[..., 1::2] = words >> 4
        vals = E2M1[nib]
    vals = vals * np.repeat(np.exp2(scales.astype(np.float64) - 127.0), 8, axis=1)[..., None]
    return vals.transpose(0, 1, 3, 2).reshape(g * 512, n)


def sigmoid(v):
    return 1.0 / (1.0 + np.exp(-v))


K, R, F, T, J, M = 512, 128, 512, 2048, 512, 256


def setup_inputs():
    n = np.random.standard_normal
    idx = np.random.permutation(T)[:J]
    idx4 = np.random.permutation(T)[:J]
    idx2 = np.stack([np.random.permutation(J)[:M] for _ in range(8)])
    idx3 = np.stack([np.random.permutation(J)[:M] for _ in range(8)])
    fk = mx_kscale(K)
    ff = mx_kscale(F)
    tabp = pack_weight(n((K, T)) / fk[:, None], "e4m3")
    tab2p = pack_weight(n((K, T)) / fk[:, None], "e4m3")
    dtabp = pack_weight(n((K, T)) / fk[:, None], "e4m3")
    return {
        "tab_words": tabp[0],
        "tab_scales": tabp[1],
        "w1": (n((K, R)) * 1 / np.sqrt(K) * fk[:, None]).astype(np.float32),
        "tab2_words": tab2p[0],
        "tab2_scales": tab2p[1],
        "w2": (n((K, R)) * 1 / np.sqrt(K) * fk[:, None]).astype(np.float32),
        "gain": (np.random.uniform(0.5, 1.5, (R, 1))).astype(np.float32),
        "wo": (n((F, R)) * 1 / np.sqrt(F) * ff[:, None]).astype(np.float32),
        "dy": (n((F, M)) / ff[:, None]).astype(np.float32),
        "dtab_words": dtabp[0],
        "dtab_scales": dtabp[1],
        "og": (np.random.uniform(0.7, 2.0, (R, 1))).astype(np.float32),
        "base": (0.3 * n((R, J))).astype(np.float32),
        "offs": striped(idx),
        "offs4": striped(idx4),
        "offs2": striped8(idx2),
        "offs3": striped8(idx3),
    }


def reference(tab_words, tab_scales, w1, tab2_words, tab2_scales, w2, gain, wo, dy, dtab_words, dtab_scales, og, base, offs, offs4, offs2, offs3):
    idx = unstriped(offs)
    idx4 = unstriped(offs4)
    idx2 = unstriped8(offs2)
    idx3 = unstriped8(offs3)
    tabu = unpack_weight(tab_words, tab_scales, "e4m3")
    tab2u = unpack_weight(tab2_words, tab2_scales, "e4m3")
    dtabu = unpack_weight(dtab_words, dtab_scales, "e4m3")
    w1q = mxq(f64(w1), 0, "e4m3")
    tabidxg = tabu[:, idx]
    a = w1q.T @ tabidxg
    dtabidxg = dtabu[:, idx]
    ta = w1q.T @ dtabidxg
    w2q = mxq(f64(w2), 0, "e4m3")
    tab2idx4g = tab2u[:, idx4]
    b = w2q.T @ tab2idx4g
    h0 = np.tanh(a)
    g1 = sigmoid(b)
    woq = mxq(f64(wo), 0, "e4m3")
    dyq = mxq(f64(dy), 0, "e4m3")
    c0 = woq.T @ dyq
    e1 = c0 * pick8(g1, idx3, 16)
    s1 = np.zeros((R, J))
    s1[np.arange(R)[:, None], idx2[np.arange(R) % 128 // 16]] = e1
    dh0 = s1 * f64(gain)
    xh0 = ta * (1.0 - np.square(h0))
    xda = xh0 * h0 * 2.0 * (-1.0) * dh0
    y = xda * f64(og) + f64(base)
    return y

@@ -1,0 +1,169 @@
+from contextlib import ExitStack
+
+import concourse.mybir as mybir
+
+K, R, F, T, J, M = 512, 128, 512, 2048, 512, 256
+FLOPS = 2 * R * (3 * K * J + F * M)
+
+F32 = mybir.dt.float32
+BF16 = mybir.dt.bfloat16
+I32 = mybir.dt.int32
+U32 = mybir.dt.uint32
+U16 = mybir.dt.uint16
+U8 = mybir.dt.uint8
+FP8X4 = mybir.dt.float8_e4m3fn_x4
+ALU = mybir.AluOpType
+ACT = mybir.ActivationFunctionType
+
+P = 128
+PACK = 4
+QUADS = 4
+
+
+def tile_attend_hvcpickgates_kernel(
+    tc, tab_words, tab_scales, w1, tab2_words, tab2_scales, w2, gain, wo, dy,
+    dtab_words, dtab_scales, og, base, offs, offs4, offs2, offs3, out,
+):
+    nc = tc.nc
+    with ExitStack() as ctx:
+        sb = ctx.enter_context(tc.tile_pool(name="sb", bufs=1))
+        ps = ctx.enter_context(tc.psum_pool(name="ps", bufs=1))
+
+        def load_list(name, src):
+            tile = sb.tile(list(src.shape), U16, name=name)
+            nc.sync.dma_start(tile[:], src)
+            return tile
+
+        def load_words(name, src):
+            tile = sb.tile([P, T], U32, name=name, align_bytes=64)
+            nc.sync.dma_start(tile[:].bitcast(I32), src[0].rearrange("p t c -> p (t c)").bitcast(I32))
+            return tile
+
+        def zeroed_scale_window(name):
+            tile = sb.tile([P, T], U8, name=name, align_bytes=64)
+            nc.vector.memset(tile[:].bitcast(I32), 0)
+            return tile
+
+        def load_scales(queue, tile, src, first_row):
+            for q in range(QUADS):
+                rows = slice(32 * q + first_row, 32 * q + first_row + 4)
+                queue.dma_start(tile[:].bitcast(I32)[rows, :], src[0, 4 * q : 4 * q + 4, :].bitcast(I32))
+
+        def load_rows(name, src):
+            tile = sb.tile([P, PACK, src.shape[1]], F32, name=name)
+            nc.sync.dma_start(tile[:], src.rearrange("(p c) w -> p c w", c=PACK))
+            return tile
+
+        def round_and_weave(name, copy, raw):
+            tile = sb.tile([P, raw.shape[2], PACK], BF16, name=name, align_bytes=64)
+            copy(tile[:], raw[:].rearrange("p c w -> p w c"))
+            return tile
+
+        def quantise(name, woven):
+            width = woven.shape[1]
+            codes = sb.tile([P, width], U32, name=name + "_codes", align_bytes=64)
+            plane = sb.tile([P, width], U8, name=name + "_plane", align_bytes=64)
+            nc.vector.quantize_mx(
+                out=codes[:].bitcast(FP8X4), scales=plane[:], in_=woven[:].rearrange("p w c -> p (w c)")
+            )
+            return codes, plane
+
+        def gather(name, window, lst, dtype):
+            tile = sb.tile([P, J], dtype, name=name, align_bytes=64)
+            nc.vector.tensor_copy(tile[:], window[:].indirect(lst[:]))
+            return tile
+
+        def product(name, stationary, codes, plane, first_row):
+            bank = ps.tile([P, codes.shape[1]], F32, name=name)
+            nc.tensor.matmul_mx(
+                out=bank[:],
+                lhsT=stationary[0][:].bitcast(FP8X4),
+                lhsT_scale=stationary[1][:],
+                rhs=codes[:].bitcast(FP8X4),
+                rhs_scale=plane[first_row:P, :],
+                start=True,
+                stop=True,
+            )
+            return bank
+
+        row_tab2, row_tab, row_dtab = 0, 4, 8
+
+        win_s2 = zeroed_scale_window("win_s2")
+        win_s1 = zeroed_scale_window("win_s1")
+        win_sd = zeroed_scale_window("win_sd")
+        s1 = sb.tile([P, J], F32, name="s1")
+        nc.gpsimd.memset(s1[:], 0.0)
+
+        list4 = load_list("list4", offs4)
+        w2_raw = load_rows("w2_raw", w2)
+        wo_raw = load_rows("wo_raw", wo)
+        load_scales(nc.sync, win_s2, tab2_scales, row_tab2)
+        dy_raw = load_rows("dy_raw", dy)
+        list1 = load_list("list1", offs)
+        load_scales(nc.sync, win_s1, tab_scales, row_tab)
+        win_w2 = load_words("win_w2", tab2_words)
+        load_scales(nc.sync, win_sd, dtab_scales, row_dtab)
+        w1_raw = load_rows("w1_raw", w1)
+        win_w1 = load_words("win_w1", tab_words)
+        list3 = load_list("list3", offs3)
+        list2 = load_list("list2", offs2)
+        win_wd = load_words("win_wd", dtab_words)
+        base_sb = sb.tile([P, J], F32, name="base_sb")
+        nc.sync.dma_start(base_sb[:], base)
+
+        gain_sb = sb.tile([P, 1], F32, name="gain_sb")
+        og_sb = sb.tile([P, 1], F32, name="og_sb")
+        nc.gpsimd.dma_start(gain_sb[:], gain)
+        nc.gpsimd.dma_start(og_sb[:], og)
+        coef = sb.tile([P, 1], F32, name="coef")
+        nc.gpsimd.tensor_scalar(coef[:], gain_sb[:], og_sb[:], 2.0, ALU.mult, ALU.mult)
+
+        w2_woven = round_and_weave("w2_woven", nc.scalar.copy, w2_raw)
+        wo_woven = round_and_weave("wo_woven", nc.scalar.copy, wo_raw)
+        dy_woven = round_and_weave("dy_woven", nc.scalar.copy, dy_raw)
+
+        tab2_plane = gather("tab2_plane", win_s2, list4, U8)
+        w2_q = quantise("w2", w2_woven)
+        wo_q = quantise("wo", wo_woven)
+        tab_plane = gather("tab_plane", win_s1, list1, U8)
+        dy_q = quantise("dy", dy_woven)
+        tab2_codes = gather("tab2_codes", win_w2, list4, U32)
+        b = product("b", w2_q, tab2_codes, tab2_plane, row_tab2)
+        g1 = sb.tile([P, J], F32, name="g1")
+        nc.scalar.activation(g1[:], b[:], ACT.Sigmoid)
+        g1_picked = sb.tile([P, M], F32, name="g1_picked")
+        nc.scalar.activation(g1_picked[:], g1[:].indirect(list3[:]), ACT.Copy)
+
+        c0 = product("c0", wo_q, dy_q[0], dy_q[1], 0)
+        c0_sb = sb.tile([P, M], F32, name="c0_sb")
+        nc.scalar.copy(c0_sb[:], c0[:])
+
+        w1_woven = round_and_weave("w1_woven", nc.vector.tensor_copy, w1_raw)
+        dtab_plane = gather("dtab_plane", win_sd, list1, U8)
+        w1_q = quantise("w1", w1_woven)
+        tab_codes = gather("tab_codes", win_w1, list1, U32)
+        a = product("a", w1_q, tab_codes, tab_plane, row_tab)
+        h0 = sb.tile([P, J], F32, name="h0")
+        nc.scalar.activation(h0[:], a[:], ACT.Tanh)
+        h0_sq = sb.tile([P, J], F32, name="h0_sq")
+        nc.scalar.activation(h0_sq[:], h0[:], ACT.Square)
+
+        nc.vector.tensor_tensor(s1[:].indirect(list2[:]), c0_sb[:], g1_picked[:], ALU.mult)
+
+        dtab_codes = gather("dtab_codes", win_wd, list1, U32)
+        ta = product("ta", w1_q, dtab_codes, dtab_plane, row_dtab)
+
+        halves = [slice(0, J // 2), slice(J // 2, J)]
+        curve = sb.tile([P, J], F32, name="curve")
+        factor = sb.tile([P, J], F32, name="factor")
+        change = sb.tile([P, J], F32, name="change")
+        result = sb.tile([P, J], F32, name="result")
+        for cols in halves:
+            nc.vector.scalar_tensor_tensor(curve[:, cols], h0_sq[:, cols], -1.0, h0[:, cols], ALU.add, ALU.mult)
+        for cols in halves:
+            nc.vector.scalar_tensor_tensor(factor[:, cols], s1[:, cols], coef[:], curve[:, cols], ALU.mult, ALU.mult)
+        for cols in halves:
+            nc.vector.tensor_tensor(change[:, cols], ta[:, cols], factor[:, cols], ALU.mult)
+        for cols in halves:
+            nc.vector.tensor_tensor(result[:, cols], change[:, cols], base_sb[:, cols], ALU.add)
+            nc.sync.dma_start(out[:, cols], result[:, cols])

@@ -35,7 +35,7 @@ def tile_attend_hvcpickgates_kernel(
             return tile
 
         def load_words(name, src):
-            tile = sb.tile([P, T], U32, name=name, align_bytes=64)
+            tile = sb.tile([P, T], U32, name=name, tag=name, align_bytes=64)
             nc.sync.dma_start(tile[:].bitcast(I32), src[0].rearrange("p t c -> p (t c)").bitcast(I32))
             return tile
 
@@ -45,9 +45,8 @@ def tile_attend_hvcpickgates_kernel(
             return tile
 
         def load_scales(queue, tile, src, first_row):
-            for q in range(QUADS):
-                rows = slice(32 * q + first_row, 32 * q + first_row + 4)
-                queue.dma_start(tile[:].bitcast(I32)[rows, :], src[0, 4 * q : 4 * q + 4, :].bitcast(I32))
+            for r in range(4):
+                queue.dma_start(tile[:].bitcast(I32)[first_row + r : P : 32, :], src[0, r:16:4, :].bitcast(I32))
 
         def load_rows(name, src):
             tile = sb.tile([P, PACK, src.shape[1]], F32, name=name)
@@ -69,18 +68,18 @@ def tile_attend_hvcpickgates_kernel(
             return codes, plane
 
         def gather(name, window, lst, dtype):
-            tile = sb.tile([P, J], dtype, name=name, align_bytes=64)
-            nc.vector.tensor_copy(tile[:], window[:].indirect(lst[:]))
+            tile = sb.tile([P, lst.shape[1] * 16], dtype, name=name, tag=name, align_bytes=64)
+            nc.vector.tensor_copy(tile[:], window[:].indirect(lst))
             return tile
 
-        def product(name, stationary, codes, plane, first_row):
+        def product(name, stationary, codes, plane):
             bank = ps.tile([P, codes.shape[1]], F32, name=name)
             nc.tensor.matmul_mx(
                 out=bank[:],
                 lhsT=stationary[0][:].bitcast(FP8X4),
                 lhsT_scale=stationary[1][:],
                 rhs=codes[:].bitcast(FP8X4),
-                rhs_scale=plane[first_row:P, :],
+                rhs_scale=plane,
                 start=True,
                 stop=True,
             )
@@ -99,11 +98,11 @@ def tile_attend_hvcpickgates_kernel(
         wo_raw = load_rows("wo_raw", wo)
         load_scales(nc.sync, win_s2, tab2_scales, row_tab2)
         dy_raw = load_rows("dy_raw", dy)
+        w1_raw = load_rows("w1_raw", w1)
         list1 = load_list("list1", offs)
         load_scales(nc.sync, win_s1, tab_scales, row_tab)
         win_w2 = load_words("win_w2", tab2_words)
         load_scales(nc.sync, win_sd, dtab_scales, row_dtab)
-        w1_raw = load_rows("w1_raw", w1)
         win_w1 = load_words("win_w1", tab_words)
         list3 = load_list("list3", offs3)
         list2 = load_list("list2", offs2)
@@ -121,40 +120,42 @@ def tile_attend_hvcpickgates_kernel(
         w2_woven = round_and_weave("w2_woven", nc.scalar.copy, w2_raw)
         wo_woven = round_and_weave("wo_woven", nc.scalar.copy, wo_raw)
         dy_woven = round_and_weave("dy_woven", nc.scalar.copy, dy_raw)
+        w1_woven = round_and_weave("w1_woven", nc.scalar.copy, w1_raw)
 
-        tab2_plane = gather("tab2_plane", win_s2, list4, U8)
+        tab2_plane = gather("tab2_plane", win_s2, list4[:], U8)
         w2_q = quantise("w2", w2_woven)
         wo_q = quantise("wo", wo_woven)
-        tab_plane = gather("tab_plane", win_s1, list1, U8)
+        tab_plane = gather("tab_plane", win_s1, list1[:], U8)
         dy_q = quantise("dy", dy_woven)
-        tab2_codes = gather("tab2_codes", win_w2, list4, U32)
-        b = product("b", w2_q, tab2_codes, tab2_plane, row_tab2)
+        w1_q = quantise("w1", w1_woven)
+        tab2_codes = gather("tab2_codes", win_w2, list4[:], U32)
+        b = product("b", w2_q, tab2_codes, tab2_plane[row_tab2:P, :])
         g1 = sb.tile([P, J], F32, name="g1")
         nc.scalar.activation(g1[:], b[:], ACT.Sigmoid)
         g1_picked = sb.tile([P, M], F32, name="g1_picked")
         nc.scalar.activation(g1_picked[:], g1[:].indirect(list3[:]), ACT.Copy)
 
-        c0 = product("c0", wo_q, dy_q[0], dy_q[1], 0)
-        c0_sb = sb.tile([P, M], F32, name="c0_sb")
+        c0 = product("c0", wo_q, dy_q[0], dy_q[1][:])
+        c0_sb = sb.tile([P, M], F32, name="c0_sb", tag="tab2_codes", align_bytes=64)
         nc.scalar.copy(c0_sb[:], c0[:])
 
-        w1_woven = round_and_weave("w1_woven", nc.vector.tensor_copy, w1_raw)
-        dtab_plane = gather("dtab_plane", win_sd, list1, U8)
-        w1_q = quantise("w1", w1_woven)
-        tab_codes = gather("tab_codes", win_w1, list1, U32)
-        a = product("a", w1_q, tab_codes, tab_plane, row_tab)
+        dtab_plane = gather("dtab_plane", win_sd, list1[:], U8)
+        halves = [slice(0, J // 2), slice(J // 2, J)]
         h0 = sb.tile([P, J], F32, name="h0")
-        nc.scalar.activation(h0[:], a[:], ACT.Tanh)
         h0_sq = sb.tile([P, J], F32, name="h0_sq")
-        nc.scalar.activation(h0_sq[:], h0[:], ACT.Square)
+        for n, cols in enumerate(halves):
+            entries = list1[:, cols.start // 16 : cols.stop // 16]
+            tab_codes = gather("tab_codes%d" % n, win_w1, entries, U32)
+            a = product("a%d" % n, w1_q, tab_codes, tab_plane[row_tab:P, cols])
+            nc.scalar.activation(h0[:, cols], a[:], ACT.Tanh)
+            nc.scalar.activation(h0_sq[:, cols], h0[:, cols], ACT.Square)
 
         nc.vector.tensor_tensor(s1[:].indirect(list2[:]), c0_sb[:], g1_picked[:], ALU.mult)
 
-        dtab_codes = gather("dtab_codes", win_wd, list1, U32)
-        ta = product("ta", w1_q, dtab_codes, dtab_plane, row_dtab)
+        dtab_codes = gather("dtab_codes", win_wd, list1[:], U32)
+        ta = product("ta", w1_q, dtab_codes, dtab_plane[row_dtab:P, :])
 
-        halves = [slice(0, J // 2), slice(J // 2, J)]
-        curve = sb.tile([P, J], F32, name="curve")
+        curve = sb.tile([P, J], F32, name="curve", tag="win_wd", align_bytes=64)
         factor = sb.tile([P, J], F32, name="factor")
         change = sb.tile([P, J], F32, name="change")
         result = sb.tile([P, J], F32, name="result")

@@ -40,7 +40,7 @@ def tile_attend_hvcpickgates_kernel(
             return tile
 
         def zeroed_scale_window(name):
-            tile = sb.tile([P, T], U8, name=name, align_bytes=64)
+            tile = sb.tile([P, T], U8, name=name, tag=name, align_bytes=64)
             nc.vector.memset(tile[:].bitcast(I32), 0)
             return tile
 
@@ -67,8 +67,8 @@ def tile_attend_hvcpickgates_kernel(
             )
             return codes, plane
 
-        def gather(name, window, lst, dtype):
-            tile = sb.tile([P, lst.shape[1] * 16], dtype, name=name, tag=name, align_bytes=64)
+        def gather(name, window, lst, dtype, tag=None):
+            tile = sb.tile([P, lst.shape[1] * 16], dtype, name=name, tag=tag or name, align_bytes=64)
             nc.vector.tensor_copy(tile[:], window[:].indirect(lst))
             return tile
 
@@ -91,7 +91,7 @@ def tile_attend_hvcpickgates_kernel(
         win_s1 = zeroed_scale_window("win_s1")
         win_sd = zeroed_scale_window("win_sd")
         s1 = sb.tile([P, J], F32, name="s1")
-        nc.gpsimd.memset(s1[:], 0.0)
+        nc.vector.memset(s1[:], 0.0)
 
         list4 = load_list("list4", offs4)
         w2_raw = load_rows("w2_raw", w2)
@@ -103,8 +103,8 @@ def tile_attend_hvcpickgates_kernel(
         load_scales(nc.sync, win_s1, tab_scales, row_tab)
         win_w2 = load_words("win_w2", tab2_words)
         load_scales(nc.sync, win_sd, dtab_scales, row_dtab)
-        win_w1 = load_words("win_w1", tab_words)
         list3 = load_list("list3", offs3)
+        win_w1 = load_words("win_w1", tab_words)
         list2 = load_list("list2", offs2)
         win_wd = load_words("win_wd", dtab_words)
         base_sb = sb.tile([P, J], F32, name="base_sb")
@@ -122,49 +122,53 @@ def tile_attend_hvcpickgates_kernel(
         dy_woven = round_and_weave("dy_woven", nc.scalar.copy, dy_raw)
         w1_woven = round_and_weave("w1_woven", nc.scalar.copy, w1_raw)
 
+        halves = [slice(0, J // 2), slice(J // 2, J)]
         tab2_plane = gather("tab2_plane", win_s2, list4[:], U8)
         w2_q = quantise("w2", w2_woven)
         wo_q = quantise("wo", wo_woven)
         tab_plane = gather("tab_plane", win_s1, list1[:], U8)
         dy_q = quantise("dy", dy_woven)
         w1_q = quantise("w1", w1_woven)
-        tab2_codes = gather("tab2_codes", win_w2, list4[:], U32)
-        b = product("b", w2_q, tab2_codes, tab2_plane[row_tab2:P, :])
         g1 = sb.tile([P, J], F32, name="g1")
-        nc.scalar.activation(g1[:], b[:], ACT.Sigmoid)
+        for n, cols in enumerate(halves):
+            entries = list4[:, cols.start // 16 : cols.stop // 16]
+            tab2_codes = gather("tab2_codes%d" % n, win_w2, entries, U32)
+            b = product("b%d" % n, w2_q, tab2_codes, tab2_plane[row_tab2:P, cols])
+            nc.scalar.activation(g1[:, cols], b[:], ACT.Sigmoid)
         g1_picked = sb.tile([P, M], F32, name="g1_picked")
         nc.scalar.activation(g1_picked[:], g1[:].indirect(list3[:]), ACT.Copy)
 
         c0 = product("c0", wo_q, dy_q[0], dy_q[1][:])
-        c0_sb = sb.tile([P, M], F32, name="c0_sb", tag="tab2_codes", align_bytes=64)
+        c0_sb = sb.tile([P, M], F32, name="c0_sb", tag="tab2_codes0", align_bytes=64)
         nc.scalar.copy(c0_sb[:], c0[:])
 
         dtab_plane = gather("dtab_plane", win_sd, list1[:], U8)
-        halves = [slice(0, J // 2), slice(J // 2, J)]
+
         h0 = sb.tile([P, J], F32, name="h0")
         h0_sq = sb.tile([P, J], F32, name="h0_sq")
-        for n, cols in enumerate(halves):
-            entries = list1[:, cols.start // 16 : cols.stop // 16]
-            tab_codes = gather("tab_codes%d" % n, win_w1, entries, U32)
-            a = product("a%d" % n, w1_q, tab_codes, tab_plane[row_tab:P, cols])
-            nc.scalar.activation(h0[:, cols], a[:], ACT.Tanh)
-            nc.scalar.activation(h0_sq[:, cols], h0[:, cols], ACT.Square)
+        tab_codes = gather("tab_codes", win_w1, list1[:], U32)
+        a = product("a", w1_q, tab_codes, tab_plane[row_tab:P, :])
+        nc.scalar.activation(h0[:], a[:], ACT.Tanh)
+        nc.scalar.activation(h0_sq[:], h0[:], ACT.Square)
 
         nc.vector.tensor_tensor(s1[:].indirect(list2[:]), c0_sb[:], g1_picked[:], ALU.mult)
+        s1_h0 = sb.tile([P, J], F32, name="s1_h0")
+        nc.gpsimd.tensor_tensor(s1_h0[:], s1[:], h0[:], ALU.mult)
 
-        dtab_codes = gather("dtab_codes", win_wd, list1[:], U32)
-        ta = product("ta", w1_q, dtab_codes, dtab_plane[row_dtab:P, :])
+        pieces = [slice(0, J // 2), slice(J // 2, 3 * J // 4), slice(3 * J // 4, J)]
+        ta = []
+        for n, cols in enumerate(pieces):
+            entries = list1[:, cols.start // 16 : cols.stop // 16]
+            dtab_codes = gather("dtab_codes%d" % n, win_wd, entries, U32)
+            ta.append(product("ta%d" % n, w1_q, dtab_codes, dtab_plane[row_dtab:P, cols]))
 
-        curve = sb.tile([P, J], F32, name="curve", tag="win_wd", align_bytes=64)
-        factor = sb.tile([P, J], F32, name="factor")
+        slope = sb.tile([P, J], F32, name="slope")
         change = sb.tile([P, J], F32, name="change")
         result = sb.tile([P, J], F32, name="result")
-        for cols in halves:
-            nc.vector.scalar_tensor_tensor(curve[:, cols], h0_sq[:, cols], -1.0, h0[:, cols], ALU.add, ALU.mult)
-        for cols in halves:
-            nc.vector.scalar_tensor_tensor(factor[:, cols], s1[:, cols], coef[:], curve[:, cols], ALU.mult, ALU.mult)
-        for cols in halves:
-            nc.vector.tensor_tensor(change[:, cols], ta[:, cols], factor[:, cols], ALU.mult)
-        for cols in halves:
+        for n, cols in enumerate(pieces):
+            nc.vector.scalar_tensor_tensor(slope[:, cols], h0_sq[:, cols], -1.0, ta[n][:], ALU.add, ALU.mult)
+        for cols in pieces:
+            nc.vector.scalar_tensor_tensor(change[:, cols], s1_h0[:, cols], coef[:], slope[:, cols], ALU.mult, ALU.mult)
+        for cols in pieces:
             nc.vector.tensor_tensor(result[:, cols], change[:, cols], base_sb[:, cols], ALU.add)
             nc.sync.dma_start(out[:, cols], result[:, cols])

@@ -39,14 +39,17 @@ def tile_attend_hvcpickgates_kernel(
             nc.sync.dma_start(tile[:].bitcast(I32), src[0].rearrange("p t c -> p (t c)").bitcast(I32))
             return tile
 
-        def zeroed_scale_window(name):
-            tile = sb.tile([P, T], U8, name=name, tag=name, align_bytes=64)
+        def zeroed_scale_window(name, width=T):
+            tile = sb.tile([P, width], U8, name=name, tag=name, align_bytes=64)
             nc.vector.memset(tile[:].bitcast(I32), 0)
             return tile
 
-        def load_scales(queue, tile, src, first_row):
+        def load_scales(tile, src):
+            nc.sync.dma_start(tile[:].bitcast(I32)[0:P:8, :], src[0].bitcast(I32))
+
+        def place_scales(plane, picked):
             for r in range(4):
-                queue.dma_start(tile[:].bitcast(I32)[first_row + r : P : 32, :], src[0, r:16:4, :].bitcast(I32))
+                nc.sync.dma_start(plane[:].bitcast(I32)[r:P:32, :], picked[:].bitcast(I32)[8 * r : P : 32, :])
 
         def load_rows(name, src):
             tile = sb.tile([P, PACK, src.shape[1]], F32, name=name)
@@ -85,30 +88,14 @@ def tile_attend_hvcpickgates_kernel(
             )
             return bank
 
-        row_tab2, row_tab, row_dtab = 0, 4, 8
-
         win_s2 = zeroed_scale_window("win_s2")
         win_s1 = zeroed_scale_window("win_s1")
         win_sd = zeroed_scale_window("win_sd")
+        tab2_plane = zeroed_scale_window("tab2_plane", J)
+        tab_plane = zeroed_scale_window("tab_plane", J)
+        dtab_plane = zeroed_scale_window("dtab_plane", J)
         s1 = sb.tile([P, J], F32, name="s1")
         nc.vector.memset(s1[:], 0.0)
-
-        list4 = load_list("list4", offs4)
-        w2_raw = load_rows("w2_raw", w2)
-        wo_raw = load_rows("wo_raw", wo)
-        load_scales(nc.sync, win_s2, tab2_scales, row_tab2)
-        dy_raw = load_rows("dy_raw", dy)
-        w1_raw = load_rows("w1_raw", w1)
-        list1 = load_list("list1", offs)
-        load_scales(nc.sync, win_s1, tab_scales, row_tab)
-        win_w2 = load_words("win_w2", tab2_words)
-        load_scales(nc.sync, win_sd, dtab_scales, row_dtab)
-        list3 = load_list("list3", offs3)
-        win_w1 = load_words("win_w1", tab_words)
-        list2 = load_list("list2", offs2)
-        win_wd = load_words("win_wd", dtab_words)
-        base_sb = sb.tile([P, J], F32, name="base_sb")
-        nc.sync.dma_start(base_sb[:], base)
 
         gain_sb = sb.tile([P, 1], F32, name="gain_sb")
         og_sb = sb.tile([P, 1], F32, name="og_sb")
@@ -117,37 +104,58 @@ def tile_attend_hvcpickgates_kernel(
         coef = sb.tile([P, 1], F32, name="coef")
         nc.gpsimd.tensor_scalar(coef[:], gain_sb[:], og_sb[:], 2.0, ALU.mult, ALU.mult)
 
+        list4 = load_list("list4", offs4)
+        w2_raw = load_rows("w2_raw", w2)
+        wo_raw = load_rows("wo_raw", wo)
+        load_scales(win_s2, tab2_scales)
+        list1 = load_list("list1", offs)
+        dy_raw = load_rows("dy_raw", dy)
+        load_scales(win_s1, tab_scales)
+        w1_raw = load_rows("w1_raw", w1)
+        win_w2 = load_words("win_w2", tab2_words)
+        load_scales(win_sd, dtab_scales)
+        list3 = load_list("list3", offs3)
+
         w2_woven = round_and_weave("w2_woven", nc.scalar.copy, w2_raw)
         wo_woven = round_and_weave("wo_woven", nc.scalar.copy, wo_raw)
         dy_woven = round_and_weave("dy_woven", nc.scalar.copy, dy_raw)
         w1_woven = round_and_weave("w1_woven", nc.scalar.copy, w1_raw)
 
         halves = [slice(0, J // 2), slice(J // 2, J)]
-        tab2_plane = gather("tab2_plane", win_s2, list4[:], U8)
+        place_scales(tab2_plane, gather("tab2_bytes", win_s2, list4[:], U8))
+        win_w1 = load_words("win_w1", tab_words)
+        list2 = load_list("list2", offs2)
         w2_q = quantise("w2", w2_woven)
         wo_q = quantise("wo", wo_woven)
-        tab_plane = gather("tab_plane", win_s1, list1[:], U8)
+        place_scales(tab_plane, gather("tab_bytes", win_s1, list1[:], U8))
+        win_wd = load_words("win_wd", dtab_words)
         dy_q = quantise("dy", dy_woven)
         w1_q = quantise("w1", w1_woven)
+        c0 = product("c0", wo_q, dy_q[0], dy_q[1][:])
         g1 = sb.tile([P, J], F32, name="g1")
-        for n, cols in enumerate(halves):
+
+        def gate_half(n):
+            cols = halves[n]
             entries = list4[:, cols.start // 16 : cols.stop // 16]
             tab2_codes = gather("tab2_codes%d" % n, win_w2, entries, U32)
-            b = product("b%d" % n, w2_q, tab2_codes, tab2_plane[row_tab2:P, cols])
+            b = product("b%d" % n, w2_q, tab2_codes, tab2_plane[:, cols])
             nc.scalar.activation(g1[:, cols], b[:], ACT.Sigmoid)
+
+        gate_half(0)
+        c0_sb = sb.tile([P, M], F32, name="c0_sb", tag="tab2_codes0", align_bytes=64)
+        nc.scalar.copy(c0_sb[:], c0[:])
+        gate_half(1)
         g1_picked = sb.tile([P, M], F32, name="g1_picked")
         nc.scalar.activation(g1_picked[:], g1[:].indirect(list3[:]), ACT.Copy)
 
-        c0 = product("c0", wo_q, dy_q[0], dy_q[1][:])
-        c0_sb = sb.tile([P, M], F32, name="c0_sb", tag="tab2_codes0", align_bytes=64)
-        nc.scalar.copy(c0_sb[:], c0[:])
-
-        dtab_plane = gather("dtab_plane", win_sd, list1[:], U8)
+        place_scales(dtab_plane, gather("dtab_bytes", win_sd, list1[:], U8))
+        base_sb = sb.tile([P, J], F32, name="base_sb")
+        nc.sync.dma_start(base_sb[:], base)
 
         h0 = sb.tile([P, J], F32, name="h0")
         h0_sq = sb.tile([P, J], F32, name="h0_sq")
         tab_codes = gather("tab_codes", win_w1, list1[:], U32)
-        a = product("a", w1_q, tab_codes, tab_plane[row_tab:P, :])
+        a = product("a", w1_q, tab_codes, tab_plane[:])
         nc.scalar.activation(h0[:], a[:], ACT.Tanh)
         nc.scalar.activation(h0_sq[:], h0[:], ACT.Square)
 
@@ -160,7 +168,7 @@ def tile_attend_hvcpickgates_kernel(
         for n, cols in enumerate(pieces):
             entries = list1[:, cols.start // 16 : cols.stop // 16]
             dtab_codes = gather("dtab_codes%d" % n, win_wd, entries, U32)
-            ta.append(product("ta%d" % n, w1_q, dtab_codes, dtab_plane[row_dtab:P, cols]))
+            ta.append(product("ta%d" % n, w1_q, dtab_codes, dtab_plane[:, cols]))
 
         slope = sb.tile([P, J], F32, name="slope")
         change = sb.tile([P, J], F32, name="change")

@@ -17,7 +17,10 @@ ACT = mybir.ActivationFunctionType
 
 P = 128
 PACK = 4
-QUADS = 4
+QUADRANT = 32
+ROWS_PER_QUADRANT = 4
+ROW_STEP = 8
+GROUP = 16
 
 
 def tile_attend_hvcpickgates_kernel(
@@ -35,129 +38,133 @@ def tile_attend_hvcpickgates_kernel(
             return tile
 
         def load_words(name, src):
-            tile = sb.tile([P, T], U32, name=name, tag=name, align_bytes=64)
+            tile = sb.tile([P, T], U32, name=name, align_bytes=64)
             nc.sync.dma_start(tile[:].bitcast(I32), src[0].rearrange("p t c -> p (t c)").bitcast(I32))
             return tile
 
-        def zeroed_scale_window(name, width=T):
-            tile = sb.tile([P, width], U8, name=name, tag=name, align_bytes=64)
+        def zeroed_bytes(name, width):
+            tile = sb.tile([P, width], U8, name=name, align_bytes=64)
             nc.vector.memset(tile[:].bitcast(I32), 0)
             return tile
 
         def load_scales(tile, src):
-            nc.sync.dma_start(tile[:].bitcast(I32)[0:P:8, :], src[0].bitcast(I32))
+            nc.sync.dma_start(tile[:].bitcast(I32)[0:P:ROW_STEP, :], src[0].bitcast(I32))
 
         def place_scales(plane, picked):
-            for r in range(4):
-                nc.sync.dma_start(plane[:].bitcast(I32)[r:P:32, :], picked[:].bitcast(I32)[8 * r : P : 32, :])
+            for r in range(ROWS_PER_QUADRANT):
+                nc.sync.dma_start(
+                    plane[:].bitcast(I32)[r:P:QUADRANT, :],
+                    picked[:].bitcast(I32)[ROW_STEP * r : P : QUADRANT, :],
+                )
 
         def load_rows(name, src):
             tile = sb.tile([P, PACK, src.shape[1]], F32, name=name)
             nc.sync.dma_start(tile[:], src.rearrange("(p c) w -> p c w", c=PACK))
             return tile
 
-        def round_and_weave(name, copy, raw):
+        def round_and_weave(name, raw):
             tile = sb.tile([P, raw.shape[2], PACK], BF16, name=name, align_bytes=64)
-            copy(tile[:], raw[:].rearrange("p c w -> p w c"))
+            nc.scalar.copy(tile[:], raw[:].rearrange("p c w -> p w c"))
             return tile
 
         def quantise(name, woven):
             width = woven.shape[1]
-            codes = sb.tile([P, width], U32, name=name + "_codes", align_bytes=64)
-            plane = sb.tile([P, width], U8, name=name + "_plane", align_bytes=64)
+            words = sb.tile([P, width], U32, name=name + "_words_q", align_bytes=64)
+            plane = sb.tile([P, width], U8, name=name + "_plane_q", align_bytes=64)
             nc.vector.quantize_mx(
-                out=codes[:].bitcast(FP8X4), scales=plane[:], in_=woven[:].rearrange("p w c -> p (w c)")
+                out=words[:].bitcast(FP8X4), scales=plane[:], in_=woven[:].rearrange("p w c -> p (w c)")
             )
-            return codes, plane
+            return words, plane
 
-        def gather(name, window, lst, dtype, tag=None):
-            tile = sb.tile([P, lst.shape[1] * 16], dtype, name=name, tag=tag or name, align_bytes=64)
-            nc.vector.tensor_copy(tile[:], window[:].indirect(lst))
+        def gather(name, window, list_tile, slots, dtype):
+            tile = sb.tile([P, slots.stop - slots.start], dtype, name=name, tag=name, align_bytes=64)
+            entries = list_tile[:, slots.start // GROUP : slots.stop // GROUP]
+            nc.vector.tensor_copy(tile[:], window[:].indirect(entries))
             return tile
 
-        def product(name, stationary, codes, plane):
-            bank = ps.tile([P, codes.shape[1]], F32, name=name)
+        def product(name, stationary, words, plane):
+            bank = ps.tile([P, words.shape[1]], F32, name=name)
             nc.tensor.matmul_mx(
                 out=bank[:],
                 lhsT=stationary[0][:].bitcast(FP8X4),
                 lhsT_scale=stationary[1][:],
-                rhs=codes[:].bitcast(FP8X4),
+                rhs=words[:].bitcast(FP8X4),
                 rhs_scale=plane,
                 start=True,
                 stop=True,
             )
             return bank
 
-        win_s2 = zeroed_scale_window("win_s2")
-        win_s1 = zeroed_scale_window("win_s1")
-        win_sd = zeroed_scale_window("win_sd")
-        tab2_plane = zeroed_scale_window("tab2_plane", J)
-        tab_plane = zeroed_scale_window("tab_plane", J)
-        dtab_plane = zeroed_scale_window("dtab_plane", J)
+        all_slots = slice(0, J)
+
+        tab2_scale_rows = zeroed_bytes("tab2_scale_rows", T)
+        tab_scale_rows = zeroed_bytes("tab_scale_rows", T)
+        dtab_scale_rows = zeroed_bytes("dtab_scale_rows", T)
+        tab2_plane = zeroed_bytes("tab2_plane", J)
+        tab_plane = zeroed_bytes("tab_plane", J)
+        dtab_plane = zeroed_bytes("dtab_plane", J)
         s1 = sb.tile([P, J], F32, name="s1")
         nc.vector.memset(s1[:], 0.0)
 
-        gain_sb = sb.tile([P, 1], F32, name="gain_sb")
-        og_sb = sb.tile([P, 1], F32, name="og_sb")
-        nc.gpsimd.dma_start(gain_sb[:], gain)
-        nc.gpsimd.dma_start(og_sb[:], og)
-        coef = sb.tile([P, 1], F32, name="coef")
-        nc.gpsimd.tensor_scalar(coef[:], gain_sb[:], og_sb[:], 2.0, ALU.mult, ALU.mult)
-
-        list4 = load_list("list4", offs4)
         w2_raw = load_rows("w2_raw", w2)
         wo_raw = load_rows("wo_raw", wo)
-        load_scales(win_s2, tab2_scales)
-        list1 = load_list("list1", offs)
+        list4 = load_list("list4", offs4)
+        load_scales(tab2_scale_rows, tab2_scales)
         dy_raw = load_rows("dy_raw", dy)
-        load_scales(win_s1, tab_scales)
+        list1 = load_list("list1", offs)
+        load_scales(tab_scale_rows, tab_scales)
         w1_raw = load_rows("w1_raw", w1)
-        win_w2 = load_words("win_w2", tab2_words)
-        load_scales(win_sd, dtab_scales)
+        tab2_all = load_words("tab2_all", tab2_words)
+        load_scales(dtab_scale_rows, dtab_scales)
         list3 = load_list("list3", offs3)
 
-        w2_woven = round_and_weave("w2_woven", nc.scalar.copy, w2_raw)
-        wo_woven = round_and_weave("wo_woven", nc.scalar.copy, wo_raw)
-        dy_woven = round_and_weave("dy_woven", nc.scalar.copy, dy_raw)
-        w1_woven = round_and_weave("w1_woven", nc.scalar.copy, w1_raw)
+        w2_woven = round_and_weave("w2_woven", w2_raw)
+        wo_woven = round_and_weave("wo_woven", wo_raw)
+        dy_woven = round_and_weave("dy_woven", dy_raw)
+        w1_woven = round_and_weave("w1_woven", w1_raw)
 
-        halves = [slice(0, J // 2), slice(J // 2, J)]
-        place_scales(tab2_plane, gather("tab2_bytes", win_s2, list4[:], U8))
-        win_w1 = load_words("win_w1", tab_words)
+        place_scales(tab2_plane, gather("tab2_bytes", tab2_scale_rows, list4, all_slots, U8))
+        tab_all = load_words("tab_all", tab_words)
         list2 = load_list("list2", offs2)
         w2_q = quantise("w2", w2_woven)
         wo_q = quantise("wo", wo_woven)
-        place_scales(tab_plane, gather("tab_bytes", win_s1, list1[:], U8))
-        win_wd = load_words("win_wd", dtab_words)
+        place_scales(tab_plane, gather("tab_bytes", tab_scale_rows, list1, all_slots, U8))
+        dtab_all = load_words("dtab_all", dtab_words)
         dy_q = quantise("dy", dy_woven)
         w1_q = quantise("w1", w1_woven)
         c0 = product("c0", wo_q, dy_q[0], dy_q[1][:])
+
         g1 = sb.tile([P, J], F32, name="g1")
 
         def gate_half(n):
-            cols = halves[n]
-            entries = list4[:, cols.start // 16 : cols.stop // 16]
-            tab2_codes = gather("tab2_codes%d" % n, win_w2, entries, U32)
-            b = product("b%d" % n, w2_q, tab2_codes, tab2_plane[:, cols])
-            nc.scalar.activation(g1[:, cols], b[:], ACT.Sigmoid)
+            slots = slice(n * J // 2, (n + 1) * J // 2)
+            tab2_picked = gather("tab2_picked%d" % n, tab2_all, list4, slots, U32)
+            b = product("b%d" % n, w2_q, tab2_picked, tab2_plane[:, slots])
+            nc.scalar.activation(g1[:, slots], b[:], ACT.Sigmoid)
 
         gate_half(0)
-        c0_sb = sb.tile([P, M], F32, name="c0_sb", tag="tab2_codes0", align_bytes=64)
+        c0_sb = sb.tile([P, M], F32, name="c0_sb", tag="tab2_picked0", align_bytes=64)
         nc.scalar.copy(c0_sb[:], c0[:])
         gate_half(1)
         g1_picked = sb.tile([P, M], F32, name="g1_picked")
         nc.scalar.activation(g1_picked[:], g1[:].indirect(list3[:]), ACT.Copy)
 
-        place_scales(dtab_plane, gather("dtab_bytes", win_sd, list1[:], U8))
+        place_scales(dtab_plane, gather("dtab_bytes", dtab_scale_rows, list1, all_slots, U8))
         base_sb = sb.tile([P, J], F32, name="base_sb")
         nc.sync.dma_start(base_sb[:], base)
+        gain_sb = sb.tile([P, 1], F32, name="gain_sb")
+        og_sb = sb.tile([P, 1], F32, name="og_sb")
+        nc.sync.dma_start(gain_sb[:], gain)
+        nc.sync.dma_start(og_sb[:], og)
 
         h0 = sb.tile([P, J], F32, name="h0")
         h0_sq = sb.tile([P, J], F32, name="h0_sq")
-        tab_codes = gather("tab_codes", win_w1, list1[:], U32)
-        a = product("a", w1_q, tab_codes, tab_plane[:])
+        tab_picked = gather("tab_picked", tab_all, list1, all_slots, U32)
+        a = product("a", w1_q, tab_picked, tab_plane[:])
         nc.scalar.activation(h0[:], a[:], ACT.Tanh)
         nc.scalar.activation(h0_sq[:], h0[:], ACT.Square)
+        gain_og = sb.tile([P, 1], F32, name="gain_og")
+        nc.scalar.activation(gain_og[:], gain_sb[:], ACT.Copy, scale=og_sb[:])
 
         nc.vector.tensor_tensor(s1[:].indirect(list2[:]), c0_sb[:], g1_picked[:], ALU.mult)
         s1_h0 = sb.tile([P, J], F32, name="s1_h0")
@@ -165,18 +172,21 @@ def tile_attend_hvcpickgates_kernel(
 
         pieces = [slice(0, J // 2), slice(J // 2, 3 * J // 4), slice(3 * J // 4, J)]
         ta = []
-        for n, cols in enumerate(pieces):
-            entries = list1[:, cols.start // 16 : cols.stop // 16]
-            dtab_codes = gather("dtab_codes%d" % n, win_wd, entries, U32)
-            ta.append(product("ta%d" % n, w1_q, dtab_codes, dtab_plane[:, cols]))
+        for n, slots in enumerate(pieces):
+            dtab_picked = gather("dtab_picked%d" % n, dtab_all, list1, slots, U32)
+            ta.append(product("ta%d" % n, w1_q, dtab_picked, dtab_plane[:, slots]))
 
-        slope = sb.tile([P, J], F32, name="slope")
-        change = sb.tile([P, J], F32, name="change")
+        minus_xh0 = sb.tile([P, J], F32, name="minus_xh0")
+        half_change = sb.tile([P, J], F32, name="half_change")
         result = sb.tile([P, J], F32, name="result")
-        for n, cols in enumerate(pieces):
-            nc.vector.scalar_tensor_tensor(slope[:, cols], h0_sq[:, cols], -1.0, ta[n][:], ALU.add, ALU.mult)
-        for cols in pieces:
-            nc.vector.scalar_tensor_tensor(change[:, cols], s1_h0[:, cols], coef[:], slope[:, cols], ALU.mult, ALU.mult)
-        for cols in pieces:
-            nc.vector.tensor_tensor(result[:, cols], change[:, cols], base_sb[:, cols], ALU.add)
-            nc.sync.dma_start(out[:, cols], result[:, cols])
+        for n, slots in enumerate(pieces):
+            nc.vector.scalar_tensor_tensor(minus_xh0[:, slots], h0_sq[:, slots], -1.0, ta[n][:], ALU.add, ALU.mult)
+        for slots in pieces:
+            nc.vector.scalar_tensor_tensor(
+                half_change[:, slots], s1_h0[:, slots], gain_og[:], minus_xh0[:, slots], ALU.mult, ALU.mult
+            )
+        for slots in pieces:
+            nc.vector.scalar_tensor_tensor(
+                result[:, slots], half_change[:, slots], 2.0, base_sb[:, slots], ALU.mult, ALU.add
+            )
+            nc.sync.dma_start(out[:, slots], result[:, slots])

from contextlib import ExitStack

import concourse.mybir as mybir

K, R, F, T, J, M = 512, 128, 512, 2048, 512, 256
FLOPS = 2 * R * (3 * K * J + F * M)

F32 = mybir.dt.float32
BF16 = mybir.dt.bfloat16
I32 = mybir.dt.int32
U32 = mybir.dt.uint32
U16 = mybir.dt.uint16
U8 = mybir.dt.uint8
FP8X4 = mybir.dt.float8_e4m3fn_x4
ALU = mybir.AluOpType
ACT = mybir.ActivationFunctionType

P = 128
PACK = 4
QUADRANT = 32
ROWS_PER_QUADRANT = 4
ROW_STEP = 8
GROUP = 16


def tile_attend_hvcpickgates_kernel(
    tc, tab_words, tab_scales, w1, tab2_words, tab2_scales, w2, gain, wo, dy,
    dtab_words, dtab_scales, og, base, offs, offs4, offs2, offs3, out,
):
    nc = tc.nc
    with ExitStack() as ctx:
        sb = ctx.enter_context(tc.tile_pool(name="sb", bufs=1))
        ps = ctx.enter_context(tc.psum_pool(name="ps", bufs=1))

        def load_list(name, src):
            tile = sb.tile(list(src.shape), U16, name=name)
            nc.sync.dma_start(tile[:], src)
            return tile

        def load_words(name, src):
            tile = sb.tile([P, T], U32, name=name, align_bytes=64)
            nc.sync.dma_start(tile[:].bitcast(I32), src[0].rearrange("p t c -> p (t c)").bitcast(I32))
            return tile

        def zeroed_bytes(name, width):
            tile = sb.tile([P, width], U8, name=name, align_bytes=64)
            nc.vector.memset(tile[:].bitcast(I32), 0)
            return tile

        def load_scales(tile, src):
            nc.sync.dma_start(tile[:].bitcast(I32)[0:P:ROW_STEP, :], src[0].bitcast(I32))

        def place_scales(plane, picked):
            for r in range(ROWS_PER_QUADRANT):
                nc.sync.dma_start(
                    plane[:].bitcast(I32)[r:P:QUADRANT, :],
                    picked[:].bitcast(I32)[ROW_STEP * r : P : QUADRANT, :],
                )

        def load_rows(name, src):
            tile = sb.tile([P, PACK, src.shape[1]], F32, name=name)
            nc.sync.dma_start(tile[:], src.rearrange("(p c) w -> p c w", c=PACK))
            return tile

        def round_and_weave(name, raw):
            tile = sb.tile([P, raw.shape[2], PACK], BF16, name=name, align_bytes=64)
            nc.scalar.copy(tile[:], raw[:].rearrange("p c w -> p w c"))
            return tile

        def quantise(name, woven):
            width = woven.shape[1]
            words = sb.tile([P, width], U32, name=name + "_words_q", align_bytes=64)
            plane = sb.tile([P, width], U8, name=name + "_plane_q", align_bytes=64)
            nc.vector.quantize_mx(
                out=words[:].bitcast(FP8X4), scales=plane[:], in_=woven[:].rearrange("p w c -> p (w c)")
            )
            return words, plane

        def gather(name, window, list_tile, slots, dtype):
            tile = sb.tile([P, slots.stop - slots.start], dtype, name=name, tag=name, align_bytes=64)
            entries = list_tile[:, slots.start // GROUP : slots.stop // GROUP]
            nc.vector.tensor_copy(tile[:], window[:].indirect(entries))
            return tile

        def product(name, stationary, words, plane):
            bank = ps.tile([P, words.shape[1]], F32, name=name)
            nc.tensor.matmul_mx(
                out=bank[:],
                lhsT=stationary[0][:].bitcast(FP8X4),
                lhsT_scale=stationary[1][:],
                rhs=words[:].bitcast(FP8X4),
                rhs_scale=plane,
                start=True,
                stop=True,
            )
            return bank

        all_slots = slice(0, J)

        tab2_scale_rows = zeroed_bytes("tab2_scale_rows", T)
        tab_scale_rows = zeroed_bytes("tab_scale_rows", T)
        dtab_scale_rows = zeroed_bytes("dtab_scale_rows", T)
        tab2_plane = zeroed_bytes("tab2_plane", J)
        tab_plane = zeroed_bytes("tab_plane", J)
        dtab_plane = zeroed_bytes("dtab_plane", J)
        s1 = sb.tile([P, J], F32, name="s1")
        nc.vector.memset(s1[:], 0.0)

        w2_raw = load_rows("w2_raw", w2)
        wo_raw = load_rows("wo_raw", wo)
        list4 = load_list("list4", offs4)
        load_scales(tab2_scale_rows, tab2_scales)
        dy_raw = load_rows("dy_raw", dy)
        list1 = load_list("list1", offs)
        load_scales(tab_scale_rows, tab_scales)
        w1_raw = load_rows("w1_raw", w1)
        tab2_all = load_words("tab2_all", tab2_words)
        load_scales(dtab_scale_rows, dtab_scales)
        list3 = load_list("list3", offs3)

        w2_woven = round_and_weave("w2_woven", w2_raw)
        wo_woven = round_and_weave("wo_woven", wo_raw)
        dy_woven = round_and_weave("dy_woven", dy_raw)
        w1_woven = round_and_weave("w1_woven", w1_raw)

        place_scales(tab2_plane, gather("tab2_bytes", tab2_scale_rows, list4, all_slots, U8))
        tab_all = load_words("tab_all", tab_words)
        list2 = load_list("list2", offs2)
        w2_q = quantise("w2", w2_woven)
        wo_q = quantise("wo", wo_woven)
        place_scales(tab_plane, gather("tab_bytes", tab_scale_rows, list1, all_slots, U8))
        dtab_all = load_words("dtab_all", dtab_words)
        dy_q = quantise("dy", dy_woven)
        w1_q = quantise("w1", w1_woven)
        c0 = product("c0", wo_q, dy_q[0], dy_q[1][:])

        g1 = sb.tile([P, J], F32, name="g1")

        def gate_half(n):
            slots = slice(n * J // 2, (n + 1) * J // 2)
            tab2_picked = gather("tab2_picked%d" % n, tab2_all, list4, slots, U32)
            b = product("b%d" % n, w2_q, tab2_picked, tab2_plane[:, slots])
            nc.scalar.activation(g1[:, slots], b[:], ACT.Sigmoid)

        gate_half(0)
        c0_sb = sb.tile([P, M], F32, name="c0_sb", tag="tab2_picked0", align_bytes=64)
        nc.scalar.copy(c0_sb[:], c0[:])
        gate_half(1)
        g1_picked = sb.tile([P, M], F32, name="g1_picked")
        nc.scalar.activation(g1_picked[:], g1[:].indirect(list3[:]), ACT.Copy)

        place_scales(dtab_plane, gather("dtab_bytes", dtab_scale_rows, list1, all_slots, U8))
        base_sb = sb.tile([P, J], F32, name="base_sb")
        nc.sync.dma_start(base_sb[:], base)
        gain_sb = sb.tile([P, 1], F32, name="gain_sb")
        og_sb = sb.tile([P, 1], F32, name="og_sb")
        nc.sync.dma_start(gain_sb[:], gain)
        nc.sync.dma_start(og_sb[:], og)

        h0 = sb.tile([P, J], F32, name="h0")
        h0_sq = sb.tile([P, J], F32, name="h0_sq")
        tab_picked = gather("tab_picked", tab_all, list1, all_slots, U32)
        a = product("a", w1_q, tab_picked, tab_plane[:])
        nc.scalar.activation(h0[:], a[:], ACT.Tanh)
        nc.scalar.activation(h0_sq[:], h0[:], ACT.Square)
        gain_og = sb.tile([P, 1], F32, name="gain_og")
        nc.scalar.activation(gain_og[:], gain_sb[:], ACT.Copy, scale=og_sb[:])

        nc.vector.tensor_tensor(s1[:].indirect(list2[:]), c0_sb[:], g1_picked[:], ALU.mult)
        s1_h0 = sb.tile([P, J], F32, name="s1_h0")
        nc.gpsimd.tensor_tensor(s1_h0[:], s1[:], h0[:], ALU.mult)

        pieces = [slice(0, J // 2), slice(J // 2, 3 * J // 4), slice(3 * J // 4, J)]
        ta = []
        for n, slots in enumerate(pieces):
            dtab_picked = gather("dtab_picked%d" % n, dtab_all, list1, slots, U32)
            ta.append(product("ta%d" % n, w1_q, dtab_picked, dtab_plane[:, slots]))

        minus_xh0 = sb.tile([P, J], F32, name="minus_xh0")
        half_change = sb.tile([P, J], F32, name="half_change")
        result = sb.tile([P, J], F32, name="result")
        for n, slots in enumerate(pieces):
            nc.vector.scalar_tensor_tensor(minus_xh0[:, slots], h0_sq[:, slots], -1.0, ta[n][:], ALU.add, ALU.mult)
        for slots in pieces:
            nc.vector.scalar_tensor_tensor(
                half_change[:, slots], s1_h0[:, slots], gain_og[:], minus_xh0[:, slots], ALU.mult, ALU.mult
            )
        for slots in pieces:
            nc.vector.scalar_tensor_tensor(
                result[:, slots], half_change[:, slots], 2.0, base_sb[:, slots], ALU.mult, ALU.add
            )
            nc.sync.dma_start(out[:, slots], result[:, slots])
